import numpy as np
import ml_dtypes


def mxq(x, axis, fmt="e4m3"):
    dtype, down = {"e4m3": (ml_dtypes.float8_e4m3fn, 7), "e5m2": (ml_dtypes.float8_e5m2, 14)}[fmt]
    v = np.moveaxis(np.asarray(x, np.float32).astype(ml_dtypes.bfloat16).astype(np.float64), axis, -1)
    blocks = v.reshape(v.shape[:-1] + (-1, 32))
    amax = np.abs(blocks).max(-1, keepdims=True)
    byte = np.maximum(np.where(amax > 0, np.frexp(amax)[1] - 1 + 127, 0) - down, 1)
    scale = np.exp2(byte - 127.0)
    codes = (blocks / scale).astype(np.float32).astype(dtype).astype(np.float64)
    return np.moveaxis((codes * scale).reshape(v.shape), -1, axis)


WIDE = False


def mx_kscale(k):
    if not WIDE:
        return np.ones(k)
    levels = np.array([10, -10, 5, -5, 0])
    if k % 512:
        return np.exp2(np.random.permutation(np.resize(levels, k // 32))).repeat(32)
    a = np.empty((k // 512, 16))
    for p in range(k // 512):
        a[p, :8] = np.random.permutation(np.resize(levels, 8))
        for g in range(8):
            far = levels[np.abs(levels - a[p, g]) >= 10]
            a[p, g + 8] = far[np.random.randint(len(far))]
    return np.exp2(a.ravel()).repeat(32)


def f64(x):
    return np.asarray(x).astype(np.float64)


def striped(idx):
    return np.tile(idx.reshape(-1, 16).T, (8, 1)).astype(np.uint16)


def unstriped(offs):
    return offs[:16].T.reshape(-1).astype(np.int64)


E2M1 = np.array([0.0, 0.5, 1.0, 1.5, 2.0, 3.0, 4.0, 6.0, -0.0, -0.5, -1.0, -1.5, -2.0, -3.0, -4.0, -6.0])


def pack_weight(w, fmt):
    k, n = w.shape
    w = f64(np.asarray(w, np.float32).astype(ml_dtypes.bfloat16)).reshape(k // 32, 32, n)
    amax = np.abs(w).max(1)
    if fmt == "e4m3":
        byte = np.frexp(amax)[1] - 1 + 127 - 7
    else:
        mant, ex = np.frexp(amax / 6.0)
        byte = np.where(mant > 0.5, ex, ex - 1) + 127
    byte = np.clip(np.where(amax > 0, byte, 1), 1, 254)
    scaled = (w * np.exp2(127.0 - byte)[:, None, :]).reshape(k, n).astype(np.float32)
    by_word = np.ascontiguousarray(scaled.reshape(k // 512, 128, 4, n).transpose(0, 1, 3, 2))
    if fmt == "e4m3":
        words = by_word.astype(ml_dtypes.float8_e4m3fn).view(np.uint8)
    else:
        c = by_word.astype(ml_dtypes.float4_e2m1fn).view(np.uint8) & 0xF
        words = (c[..., 0::2] | (c[..., 1::2] << 4)).reshape(k // 512, 128, 2 * n)
    return np.ascontiguousarray(words), np.ascontiguousarray(byte.astype(np.uint8).reshape(k // 512, 16, n))


def unpack_weight(words, scales, fmt):
    g, _, n = scales.shape
    words = np.ascontiguousarray(words).reshape(g, 128, n, -1)
    if fmt == "e4m3":
        vals = words.view(ml_dtypes.float8_e4m3fn).astype(np.float64)
    else:
        nib = np.empty((g, 128, n, 4), np.uint8)
        nib[..., 0::2] = words & 0xF
        nib[..., 1::2] = words >> 4
        vals = E2M1[nib]
    vals = vals * np.repeat(np.exp2(scales.astype(np.float64) - 127.0), 8, axis=1)[..., None]
    return vals.transpose(0, 1, 3, 2).reshape(g * 512, n)


def gelu(v):
    return 0.5 * v * (1.0 + np.tanh(np.sqrt(2.0 / np.pi) * (v + 0.044715 * v**3)))


def bf(x):
    return np.asarray(x, np.float32).astype(ml_dtypes.bfloat16)


def planes(Y):
    n, m = Y.shape
    b = f64(bf(Y)).reshape(n // 32, 32, m)
    amax = np.abs(b).max(1)
    byte = np.clip(np.where(amax > 0, np.frexp(amax)[1] - 1 + 127 - 7, 1), 1, 254)
    codes = (b * np.exp2(127.0 - byte)[:, None, :]).reshape(n, m).astype(np.float32).astype(ml_dtypes.float8_e4m3fn).view(np.uint8)
    words = codes.reshape(n // 512, 128, 4, m).transpose(0, 1, 3, 2)
    return np.ascontiguousarray(words), np.ascontiguousarray(byte.astype(np.uint8).reshape(n // 512, 16, m))


K, H, N, T, S, P = 1024, 1024, 1024, 4096, 1024, 512

def setup_inputs():
    n = np.random.standard_normal
    s = mx_kscale(K)[:, None]
    u = mx_kscale(H)[:, None]
    tab_words, tab_scales = pack_weight(n((K, T)) * s, "e4m3")
    w2_words, w2_scales = pack_weight(0.75 * n((K, H)) / np.sqrt(K) / s * u.T, "e2m1")
    size = np.exp(0.8 * n(N))
    return {
        "tab_words": tab_words, "tab_scales": tab_scales,
        "offs": striped(np.random.permutation(T)[:S]),
        "pos1": striped(np.random.permutation(S)[:P]),
        "pos2": striped(np.random.permutation(S)[:P]),
        "w1": (0.75 * n((K, H)) / np.sqrt(K) / s).astype(np.float32),
        "base": (0.55 * n((H, S))).astype(np.float32),
        "w2_words": w2_words, "w2_scales": w2_scales,
        "gain": (np.random.uniform(1.0, 2.2, H) * u[:, 0]).astype(np.float32),
        "steep": np.random.uniform(0.6, 3.0, H).astype(np.float32),
        "thr": n(H).astype(np.float32),
        "pref": (0.4 * n((H, P))).astype(np.float32),
        "w3": (n((H, N)) / np.sqrt(H) / u * size[None, :]).astype(np.float32),
        "bias": (0.5 * n(N) * size).astype(np.float32),
    }

def reference(tab_words, tab_scales, offs, pos1, pos2, w1, base, w2_words, w2_scales,
              gain, steep, thr, pref, w3, bias):
    v = unpack_weight(tab_words, tab_scales, "e4m3")[:, unstriped(offs)]
    h = (mxq(f64(w1), 0, "e4m3").T @ v) + f64(base)
    g = (unpack_weight(w2_words, w2_scales, "e2m1").T @ v) + f64(gain)[:, None] * np.tanh(h)
    a = 1.0 / (1.0 + np.exp(-(f64(steep)[:, None] * h[:, unstriped(pos1)] + f64(thr)[:, None])))
    f = (a - f64(pref)) * g[:, unstriped(pos2)]
    y = (mxq(f64(w3), 0, "e4m3").T @ mxq(f, 0, "e4m3")) + f64(bias)[:, None]
    words, scales = planes(y)
    return y, words, scales

@@ -1,0 +1,273 @@
+from contextlib import ExitStack
+
+import concourse.mybir as mybir
+
+K, H, N, T, S, M = 1024, 1024, 1024, 4096, 1024, 512
+FLOPS = 2 * (2 * K * H * S + H * N * M)
+
+F32 = mybir.dt.float32
+BF16 = mybir.dt.bfloat16
+I32 = mybir.dt.int32
+U32 = mybir.dt.uint32
+U16 = mybir.dt.uint16
+U8 = mybir.dt.uint8
+FP8X4 = mybir.dt.float8_e4m3fn_x4
+FP4X4 = mybir.dt.float4_e2m1fn_x4
+ACT = mybir.ActivationFunctionType
+ALU = mybir.AluOpType
+
+P = 128
+PACK = 4
+PASS = P * PACK
+PASSES = 2
+BANK = 512
+QUADS = 4
+
+
+def tile_list_carer_rota_match_kernel(
+    tc, tab_words, tab_scales, offs, pos1, pos2, w1, base, w2_words, w2_scales,
+    gain, steep, thr, pref, w3, bias, out_0, out_1, out_2,
+):
+    nc = tc.nc
+    with ExitStack() as ctx:
+        keep = ctx.enter_context(tc.tile_pool(name="keep", bufs=1))
+        ring = ctx.enter_context(tc.tile_pool(name="ring", bufs=2))
+        psum = ctx.enter_context(tc.psum_pool(name="psum", bufs=8))
+
+        offs_sb = keep.tile([P, S // 16], U16, name="offs_sb")
+        pos1_sb = keep.tile([P, M // 16], U16, name="pos1_sb")
+        pos2_sb = keep.tile([P, M // 16], U16, name="pos2_sb")
+        tab_w = [keep.tile([P, T], U32, name="tab_w%d" % a) for a in range(PASSES)]
+        tab_s = keep.tile([P, PASSES, T], U8, name="tab_s")
+        v_w = [keep.tile([P, S], U32, name="v_w%d" % a, align_bytes=64) for a in range(PASSES)]
+        v_s = [keep.tile([P, S], U8, name="v_s%d" % a, align_bytes=64) for a in range(PASSES)]
+        w2_w_raw = keep.tile([P, PASSES, 2 * H], U8, name="w2_w_raw")
+        w2_s_raw = keep.tile([P, PASSES, H], U8, name="w2_s_raw")
+        w2_w = keep.tile([P, PASSES, 2 * H], U8, name="w2_w", align_bytes=64)
+        w2_s = keep.tile([P, PASSES, H], U8, name="w2_s", align_bytes=64)
+        rowvec = {}
+        for name in ("gain", "steep", "thr", "bias"):
+            rowvec[name] = keep.tile([P, PASSES * PACK], F32, name=name + "_sb")
+
+        def plane_rows(tile, dram, q):
+            sb = tile[32 * q : 32 * q + 4, :, :].bitcast(I32)
+            return sb, dram[:, 4 * q : 4 * q + 4, :].bitcast(I32).rearrange("a r n -> r a n")
+
+        def load_weight(w, k_group, col_group):
+            raw = ring.tile([P, PACK, PASS], F32, name="raw", tag="raw", bufs=4)
+            rows = w[k_group * PASS : (k_group + 1) * PASS, col_group * PASS : (col_group + 1) * PASS]
+            nc.sync.dma_start(out=raw[:], in_=rows.rearrange("(p j) c -> p j c", j=PACK))
+            return raw
+
+        def round_weight(copy, rounded, raw, m0, m1):
+            copy(
+                out=rounded[:].rearrange("p (t m j) -> p m j t", t=PACK, j=PACK)[:, m0:m1],
+                in_=raw[:].rearrange("p j (m t) -> p m j t", t=PACK)[:, m0:m1],
+            )
+
+        def rounded_tile():
+            return ring.tile([P, PACK * PASS], BF16, name="rounded", tag="rounded", bufs=3, align_bytes=64)
+
+        def quantize(name, rounded):
+            codes = keep.tile([P, PASS], U32, name=name + "_w", align_bytes=64)
+            scales = keep.tile([P, PASS], U8, name=name + "_s", align_bytes=64)
+            nc.vector.quantize_mx(out=codes[:].bitcast(FP8X4), scales=scales[:], in_=rounded[:])
+            return codes, scales
+
+        base_rows = base.rearrange("(b p t) n -> b t p n", p=P, t=PACK)
+        pref_rows = pref.rearrange("(b p t) n -> b t p n", p=P, t=PACK)
+        base_sb, diff, picked = {}, {}, {}
+
+        def load_rows(i):
+            b, t = divmod(i, PACK)
+            base_sb[i] = ring.tile([P, S], F32, name="base_sb", tag="base_sb", bufs=4)
+            nc.sync.dma_start(out=base_sb[i][:], in_=base_rows[b, t])
+            if t == 0:
+                diff[b] = ring.tile([P, PACK, M], F32, name="diff", tag="group", bufs=4)
+                picked[b] = ring.tile([P, PACK, M], F32, name="picked", tag="group", bufs=4)
+            nc.sync.dma_start(out=diff[b][:, t, :], in_=pref_rows[b, t])
+
+        nc.vector.memset(tab_s[:].bitcast(I32), 0)
+        nc.gpsimd.memset(w2_s_raw[:].bitcast(I32), 0)
+        nc.sync.dma_start(offs_sb[:], offs)
+        nc.sync.dma_start(pos1_sb[:], pos1)
+        nc.sync.dma_start(pos2_sb[:], pos2)
+        for name, vec in (("gain", gain), ("steep", steep), ("thr", thr), ("bias", bias)):
+            nc.sync.dma_start(
+                out=rowvec[name][:].rearrange("p (b t) -> p b t", t=PACK),
+                in_=vec.rearrange("(b p t) -> p b t", p=P, t=PACK),
+            )
+        nc.sync.dma_start(out=tab_w[0][:].bitcast(I32), in_=tab_words[0].rearrange("p t i -> p (t i)").bitcast(I32))
+        for q in range(QUADS):
+            sb, dram = plane_rows(tab_s, tab_scales, q)
+            nc.sync.dma_start(out=sb, in_=dram)
+        raw00 = load_weight(w1, 0, 0)
+        nc.sync.dma_start(out=w2_w_raw[:].bitcast(I32), in_=w2_words.bitcast(I32).rearrange("a p n -> p a n"))
+        for q in range(QUADS):
+            sb, dram = plane_rows(w2_s_raw, w2_scales, q)
+            nc.sync.dma_start(out=sb, in_=dram)
+        nc.sync.dma_start(out=tab_w[1][:].bitcast(I32), in_=tab_words[1].rearrange("p t i -> p (t i)").bitcast(I32))
+        raw10 = load_weight(w1, 1, 0)
+        load_rows(0)
+        load_rows(1)
+
+        w1_q, w3_q, f_q = {}, {}, {}
+        nc.vector.tensor_copy(v_w[0][:], tab_w[0][:].indirect(offs_sb[:]))
+        rounded = rounded_tile()
+        round_weight(nc.scalar.copy, rounded, raw00, 0, P)
+        for a in range(PASSES):
+            nc.vector.tensor_copy(v_s[a][:], tab_s[:, a, :].indirect(offs_sb[:]))
+        w1_q[0, 0] = quantize("w1_00", rounded)
+        nc.vector.tensor_copy(
+            out=w2_w[:].bitcast(U16).rearrange("p a (b t m) -> p (a b) t m", t=PACK, m=P),
+            in_=w2_w_raw[:].bitcast(U16).rearrange("p a (b m t) -> p (a b) t m", t=PACK, m=P),
+        )
+        nc.vector.tensor_copy(
+            out=w2_s[:].rearrange("p a (b t m) -> p (a b) t m", t=PACK, m=P),
+            in_=w2_s_raw[:].rearrange("p a (b m t) -> p (a b) t m", t=PACK, m=P),
+        )
+        nc.vector.tensor_copy(v_w[1][:], tab_w[1][:].indirect(offs_sb[:]))
+        rounded = rounded_tile()
+        round_weight(nc.scalar.copy, rounded, raw10, 0, 44)
+        round_weight(nc.vector.tensor_copy, rounded, raw10, 44, P)
+        w1_q[1, 0] = quantize("w1_10", rounded)
+
+        later = [(w1_q, "w1", w1, a, 1) for a in range(PASSES)]
+        later = later + [(w3_q, "w3", w3, b, g) for g in range(PASSES) for b in range(PASSES)]
+        later_raw = {}
+
+        def load_later(n):
+            store, name, w, k_group, col_group = later[n]
+            later_raw[n] = load_weight(w, k_group, col_group)
+
+        def prepare_later(n):
+            store, name, w, k_group, col_group = later[n]
+            rounded = rounded_tile()
+            round_weight(nc.scalar.copy, rounded, later_raw[n], 0, P // 2)
+            round_weight(nc.scalar.copy, rounded, later_raw[n], P // 2, P)
+            store[k_group, col_group] = quantize("%s_%d%d" % (name, k_group, col_group), rounded)
+
+        h, tanh_h, look, g_sums = {}, {}, {}, {}
+
+        def first_products(i):
+            b, t = divmod(i, PACK)
+            cols = slice(t * P, (t + 1) * P)
+            h[i] = ring.tile([P, S], F32, name="h", tag="h", bufs=2)
+            h_sums = []
+            g_sums[i] = []
+            for half in range(S // BANK):
+                n = slice(half * BANK, (half + 1) * BANK)
+                acc = psum.tile([P, BANK], F32, name="acc", tag="acc")
+                for a in range(PASSES):
+                    codes, scales = w1_q[a, b]
+                    nc.tensor.matmul_mx(
+                        out=acc[:], lhsT=codes[:, cols].bitcast(FP8X4), lhsT_scale=scales[:, cols],
+                        rhs=v_w[a][:, n].bitcast(FP8X4), rhs_scale=v_s[a][:, n],
+                        start=(a == 0), stop=(a == PASSES - 1),
+                    )
+                h_sums.append(acc)
+            for half in range(S // BANK):
+                n = slice(half * BANK, (half + 1) * BANK)
+                acc = psum.tile([P, BANK], F32, name="acc", tag="acc")
+                for a in range(PASSES):
+                    nc.tensor.matmul_mx(
+                        out=acc[:], lhsT=w2_w[:, a, 2 * P * i : 2 * P * (i + 1)].bitcast(FP4X4),
+                        lhsT_scale=w2_s[:, a, P * i : P * (i + 1)],
+                        rhs=v_w[a][:, n].bitcast(FP8X4), rhs_scale=v_s[a][:, n],
+                        start=(a == 0), stop=(a == PASSES - 1),
+                    )
+                g_sums[i].append(acc)
+            for half in range(S // BANK):
+                n = slice(half * BANK, (half + 1) * BANK)
+                nc.vector.tensor_tensor(h[i][:, n], h_sums[half][:], base_sb[i][:, n], ALU.add)
+            tanh_h[i] = ring.tile([P, S], F32, name="tanh_h", tag="tanh_h", bufs=2)
+            nc.scalar.activation(out=tanh_h[i][:], in_=h[i][:], func=ACT.Tanh)
+            look[i] = ring.tile([P, M], F32, name="look", tag="look", bufs=2)
+            nc.scalar.activation(
+                out=look[i][:], in_=h[i][:].indirect(pos1_sb[:]), func=ACT.Sigmoid,
+                bias=rowvec["thr"][:, i : i + 1], scale=rowvec["steep"][:, i : i + 1],
+            )
+
+        def pair_terms(i):
+            b, t = divmod(i, PACK)
+            g = ring.tile([P, S], F32, name="g", tag="g", bufs=2)
+            for half in range(S // BANK):
+                n = slice(half * BANK, (half + 1) * BANK)
+                nc.vector.scalar_tensor_tensor(
+                    g[:, n], tanh_h[i][:, n], rowvec["gain"][:, i : i + 1], g_sums[i][half][:], ALU.mult, ALU.add
+                )
+            nc.vector.tensor_tensor(diff[b][:, t, :], look[i][:], diff[b][:, t, :], ALU.subtract)
+            nc.vector.tensor_copy(picked[b][:, t, :], g[:].indirect(pos2_sb[:]))
+
+        def by_lines(ap_t_m):
+            return ap_t_m.rearrange("p t (c i) -> p c t i", i=PACK)
+
+        def woven(rounded):
+            return rounded[:].rearrange("p (c i t) -> p c t i", i=PACK, t=PACK)
+
+        def quantize_f(b):
+            rounded = rounded_tile()
+            nc.vector.tensor_tensor(woven(rounded), by_lines(diff[b][:]), by_lines(picked[b][:]), ALU.mult)
+            f_q[b] = quantize("f_%d" % b, rounded)
+
+        tiles = H // P
+        load_later(0)
+        load_later(1)
+        for i in range(tiles):
+            if i + 2 < tiles:
+                load_rows(i + 2)
+            if 1 <= i <= 4:
+                load_later(i + 1)
+            first_products(i)
+            if i >= 1:
+                pair_terms(i - 1)
+            if i == PACK:
+                quantize_f(0)
+            if i < 2:
+                prepare_later(i)
+            if 3 <= i < 7:
+                prepare_later(i - 1)
+
+        y_sums = {}
+
+        def last_pass(g, t, b):
+            cols = slice(t * P, (t + 1) * P)
+            if b == 0:
+                y_sums[g, t] = psum.tile([P, BANK], F32, name="acc", tag="acc")
+            codes, scales = w3_q[b, g]
+            nc.tensor.matmul_mx(
+                out=y_sums[g, t][:], lhsT=codes[:, cols].bitcast(FP8X4), lhsT_scale=scales[:, cols],
+                rhs=f_q[b][0][:].bitcast(FP8X4), rhs_scale=f_q[b][1][:],
+                start=(b == 0), stop=(b == PASSES - 1),
+            )
+
+        for t in range(PACK):
+            last_pass(0, t, 0)
+        pair_terms(tiles - 1)
+        for t in range(PACK):
+            last_pass(1, t, 0)
+        quantize_f(1)
+        y_rows = out_0.rearrange("(g p t) m -> g p t m", p=P, t=PACK)
+        y_scales = keep.tile([P, PASSES, M], U8, name="y_scales", align_bytes=64)
+        for g in range(PASSES):
+            y = ring.tile([P, PACK, M], F32, name="y", tag="group", bufs=4)
+            for t in range(PACK):
+                last_pass(g, t, 1)
+                col = rowvec["bias"][:, PACK * g + t : PACK * g + t + 1]
+                if g == 0 and t % 2 == 1:
+                    nc.vector.tensor_scalar_add(y[:, t, :], y_sums[g, t][:], col)
+                else:
+                    nc.scalar.activation(out=y[:, t, :], in_=y_sums[g, t][:], func=ACT.Identity, bias=col)
+                if t % 2 == 1:
+                    nc.sync.dma_start(out=y_rows[g][:, t - 1 : t + 1, :], in_=y[:, t - 1 : t + 1, :])
+            rounded = rounded_tile()
+            nc.vector.tensor_copy(out=woven(rounded), in_=by_lines(y[:]))
+            y_codes = keep.tile([P, M], U32, name="y_codes%d" % g, align_bytes=64)
+            nc.vector.quantize_mx(out=y_codes[:].bitcast(FP8X4), scales=y_scales[:, g, :], in_=rounded[:])
+            nc.sync.dma_start(
+                out=out_1[g].rearrange("p m t -> p (m t)").bitcast(I32), in_=y_codes[:].bitcast(I32)
+            )
+        for q in range(QUADS):
+            sb, dram = plane_rows(y_scales, out_2, q)
+            engine = nc.scalar if q % 2 == 0 else nc.sync
+            engine.dma_start(out=dram, in_=sb)

@@ -22,6 +22,7 @@ PASS = P * PACK
 PASSES = 2
 BANK = 512
 QUADS = 4
+SCALAR_SHARE = 176
 
 
 def tile_list_carer_rota_match_kernel(
@@ -38,10 +39,11 @@ def tile_list_carer_rota_match_kernel(
         pos1_sb = keep.tile([P, M // 16], U16, name="pos1_sb")
         pos2_sb = keep.tile([P, M // 16], U16, name="pos2_sb")
         tab_w = [keep.tile([P, T], U32, name="tab_w%d" % a) for a in range(PASSES)]
-        tab_s = keep.tile([P, PASSES, T], U8, name="tab_s")
+        tab_s = keep.tile([P, T], U8, name="tab_s")
         v_w = [keep.tile([P, S], U32, name="v_w%d" % a, align_bytes=64) for a in range(PASSES)]
-        v_s = [keep.tile([P, S], U8, name="v_s%d" % a, align_bytes=64) for a in range(PASSES)]
-        w2_w_raw = keep.tile([P, PASSES, 2 * H], U8, name="w2_w_raw")
+        v_s = keep.tile([P, S], U8, name="v_s", align_bytes=64)
+        v_s_low = keep.tile([P, S], U8, name="v_s_low", align_bytes=64)
+        w2_w_raw = [keep.tile([P, PASSES, 2 * PASS], U8, name="w2_w_raw%d" % b) for b in range(PASSES)]
         w2_s_raw = keep.tile([P, PASSES, H], U8, name="w2_s_raw")
         w2_w = keep.tile([P, PASSES, 2 * H], U8, name="w2_w", align_bytes=64)
         w2_s = keep.tile([P, PASSES, H], U8, name="w2_s", align_bytes=64)
@@ -49,9 +51,9 @@ def tile_list_carer_rota_match_kernel(
         for name in ("gain", "steep", "thr", "bias"):
             rowvec[name] = keep.tile([P, PASSES * PACK], F32, name=name + "_sb")
 
-        def plane_rows(tile, dram, q):
-            sb = tile[32 * q : 32 * q + 4, :, :].bitcast(I32)
-            return sb, dram[:, 4 * q : 4 * q + 4, :].bitcast(I32).rearrange("a r n -> r a n")
+        def plane_rows(tile, dram, r):
+            sb = tile[r:P:32, :, :].bitcast(I32)
+            return sb, dram[:, r : 16 : 4, :].bitcast(I32).rearrange("a q n -> q a n")
 
         def load_weight(w, k_group, col_group):
             raw = ring.tile([P, PACK, PASS], F32, name="raw", tag="raw", bufs=4)
@@ -66,7 +68,7 @@ def tile_list_carer_rota_match_kernel(
             )
 
         def rounded_tile():
-            return ring.tile([P, PACK * PASS], BF16, name="rounded", tag="rounded", bufs=3, align_bytes=64)
+            return ring.tile([P, PACK * PASS], BF16, name="rounded", tag="rounded", bufs=4, align_bytes=64)
 
         def quantize(name, rounded):
             codes = keep.tile([P, PASS], U32, name=name + "_w", align_bytes=64)
@@ -76,61 +78,86 @@ def tile_list_carer_rota_match_kernel(
 
         base_rows = base.rearrange("(b p t) n -> b t p n", p=P, t=PACK)
         pref_rows = pref.rearrange("(b p t) n -> b t p n", p=P, t=PACK)
-        base_sb, diff, picked = {}, {}, {}
+        base_sb, diff, f_sb = {}, {}, {}
 
-        def load_rows(i):
+        def load_base(i):
             b, t = divmod(i, PACK)
             base_sb[i] = ring.tile([P, S], F32, name="base_sb", tag="base_sb", bufs=4)
             nc.sync.dma_start(out=base_sb[i][:], in_=base_rows[b, t])
-            if t == 0:
-                diff[b] = ring.tile([P, PACK, M], F32, name="diff", tag="group", bufs=4)
-                picked[b] = ring.tile([P, PACK, M], F32, name="picked", tag="group", bufs=4)
-            nc.sync.dma_start(out=diff[b][:, t, :], in_=pref_rows[b, t])
 
-        nc.vector.memset(tab_s[:].bitcast(I32), 0)
-        nc.gpsimd.memset(w2_s_raw[:].bitcast(I32), 0)
-        nc.sync.dma_start(offs_sb[:], offs)
-        nc.sync.dma_start(pos1_sb[:], pos1)
-        nc.sync.dma_start(pos2_sb[:], pos2)
-        for name, vec in (("gain", gain), ("steep", steep), ("thr", thr), ("bias", bias)):
+        def load_pref(i):
+            b, t = divmod(i, PACK)
+            diff[i] = ring.tile([P, M], F32, name="diff", tag="diff", bufs=4)
+            nc.sync.dma_start(out=diff[i][:], in_=pref_rows[b, t])
+
+        def load_rows(i):
+            load_base(i)
+            load_pref(i)
+
+        def load_vector(name, vec):
             nc.sync.dma_start(
                 out=rowvec[name][:].rearrange("p (b t) -> p b t", t=PACK),
                 in_=vec.rearrange("(b p t) -> p b t", p=P, t=PACK),
             )
-        nc.sync.dma_start(out=tab_w[0][:].bitcast(I32), in_=tab_words[0].rearrange("p t i -> p (t i)").bitcast(I32))
-        for q in range(QUADS):
-            sb, dram = plane_rows(tab_s, tab_scales, q)
-            nc.sync.dma_start(out=sb, in_=dram)
-        raw00 = load_weight(w1, 0, 0)
-        nc.sync.dma_start(out=w2_w_raw[:].bitcast(I32), in_=w2_words.bitcast(I32).rearrange("a p n -> p a n"))
-        for q in range(QUADS):
-            sb, dram = plane_rows(w2_s_raw, w2_scales, q)
-            nc.sync.dma_start(out=sb, in_=dram)
-        nc.sync.dma_start(out=tab_w[1][:].bitcast(I32), in_=tab_words[1].rearrange("p t i -> p (t i)").bitcast(I32))
-        raw10 = load_weight(w1, 1, 0)
-        load_rows(0)
-        load_rows(1)
 
-        w1_q, w3_q, f_q = {}, {}, {}
+        def load_table(a):
+            nc.sync.dma_start(
+                out=tab_w[a][:].bitcast(I32), in_=tab_words[a].rearrange("p t i -> p (t i)").bitcast(I32)
+            )
+
+        def load_w2_words(b):
+            cols = slice(b * PASS // 2, (b + 1) * PASS // 2)
+            nc.sync.dma_start(
+                out=w2_w_raw[b][:].bitcast(I32), in_=w2_words.bitcast(I32).rearrange("a p n -> p a n")[:, :, cols]
+            )
+
+        nc.vector.memset(tab_s[:].bitcast(I32), 0)
+        nc.vector.memset(w2_s_raw[:].bitcast(I32), 0)
+        nc.vector.memset(v_s_low[:].bitcast(I32), 0)
+        for r in range(QUADS):
+            sb, dram = plane_rows(w2_s_raw, w2_scales, r)
+            nc.gpsimd.dma_start(out=sb, in_=dram)
+        nc.sync.dma_start(offs_sb[:], offs)
+        nc.sync.dma_start(pos1_sb[:], pos1)
+        nc.sync.dma_start(pos2_sb[:], pos2)
+        for name, vec in (("gain", gain), ("steep", steep), ("thr", thr), ("bias", bias)):
+            load_vector(name, vec)
+        load_table(0)
+        for q in range(QUADS):
+            nc.sync.dma_start(
+                out=tab_s[32 * q : 32 * q + 8, :].bitcast(I32), in_=tab_scales[:, 4 * q : 4 * q + 4, :].bitcast(I32)
+            )
+        load_table(1)
+        raw00 = load_weight(w1, 0, 0)
+        raw10 = load_weight(w1, 1, 0)
+        load_base(0)
+        load_w2_words(0)
+        load_base(1)
+        load_pref(0)
+        load_pref(1)
+
+        w1_q, w3_q = {}, {}
         nc.vector.tensor_copy(v_w[0][:], tab_w[0][:].indirect(offs_sb[:]))
-        rounded = rounded_tile()
-        round_weight(nc.scalar.copy, rounded, raw00, 0, P)
-        for a in range(PASSES):
-            nc.vector.tensor_copy(v_s[a][:], tab_s[:, a, :].indirect(offs_sb[:]))
-        w1_q[0, 0] = quantize("w1_00", rounded)
-        nc.vector.tensor_copy(
-            out=w2_w[:].bitcast(U16).rearrange("p a (b t m) -> p (a b) t m", t=PACK, m=P),
-            in_=w2_w_raw[:].bitcast(U16).rearrange("p a (b m t) -> p (a b) t m", t=PACK, m=P),
-        )
-        nc.vector.tensor_copy(
-            out=w2_s[:].rearrange("p a (b t m) -> p (a b) t m", t=PACK, m=P),
-            in_=w2_s_raw[:].rearrange("p a (b m t) -> p (a b) t m", t=PACK, m=P),
-        )
+        nc.vector.tensor_copy(v_s[:], tab_s[:].indirect(offs_sb[:]))
+        for r in range(QUADS):
+            nc.gpsimd.dma_start(out=v_s_low[r:P:32, :].bitcast(I32), in_=v_s[4 + r : P : 32, :].bitcast(I32))
         nc.vector.tensor_copy(v_w[1][:], tab_w[1][:].indirect(offs_sb[:]))
-        rounded = rounded_tile()
-        round_weight(nc.scalar.copy, rounded, raw10, 0, 44)
-        round_weight(nc.vector.tensor_copy, rounded, raw10, 44, P)
-        w1_q[1, 0] = quantize("w1_10", rounded)
+        for a, raw, split in ((0, raw00, 64), (1, raw10, 44)):
+            rounded = rounded_tile()
+            round_weight(nc.scalar.copy, rounded, raw, 0, split)
+            round_weight(nc.vector.tensor_copy, rounded, raw, split, P)
+            w1_q[a, 0] = quantize("w1_%d0" % a, rounded)
+
+        def deal_w2(b):
+            cols = slice(b * PASS, (b + 1) * PASS)
+            nc.scalar.copy(
+                out=w2_w[:].bitcast(U16)[:, :, cols].rearrange("p a (t m) -> p a t m", t=PACK),
+                in_=w2_w_raw[b][:].bitcast(U16).rearrange("p a (m t) -> p a t m", t=PACK),
+            )
+            nc.vector.tensor_copy(
+                out=w2_s[:, :, cols].rearrange("p a (t m) -> p a t m", t=PACK),
+                in_=w2_s_raw[:, :, cols].rearrange("p a (m t) -> p a t m", t=PACK),
+            )
 
         later = [(w1_q, "w1", w1, a, 1) for a in range(PASSES)]
         later = later + [(w3_q, "w3", w3, b, g) for g in range(PASSES) for b in range(PASSES)]
@@ -149,10 +176,17 @@ def tile_list_carer_rota_match_kernel(
 
         h, tanh_h, look, g_sums = {}, {}, {}, {}
 
+        def take_look(i):
+            look[i] = ring.tile([P, M], F32, name="look", tag="look", bufs=3)
+            nc.scalar.activation(
+                out=look[i][:], in_=h[i][:].indirect(pos1_sb[:]), func=ACT.Sigmoid,
+                bias=rowvec["thr"][:, i : i + 1], scale=rowvec["steep"][:, i : i + 1],
+            )
+
         def first_products(i):
             b, t = divmod(i, PACK)
             cols = slice(t * P, (t + 1) * P)
-            h[i] = ring.tile([P, S], F32, name="h", tag="h", bufs=2)
+            h[i] = ring.tile([P, S], F32, name="h", tag="h", bufs=3)
             h_sums = []
             g_sums[i] = []
             for half in range(S // BANK):
@@ -162,10 +196,12 @@ def tile_list_carer_rota_match_kernel(
                     codes, scales = w1_q[a, b]
                     nc.tensor.matmul_mx(
                         out=acc[:], lhsT=codes[:, cols].bitcast(FP8X4), lhsT_scale=scales[:, cols],
-                        rhs=v_w[a][:, n].bitcast(FP8X4), rhs_scale=v_s[a][:, n],
+                        rhs=v_w[a][:, n].bitcast(FP8X4), rhs_scale=v_s[4 * a : P, n],
                         start=(a == 0), stop=(a == PASSES - 1),
                     )
                 h_sums.append(acc)
+            if t == 0:
+                deal_w2(b)
             for half in range(S // BANK):
                 n = slice(half * BANK, (half + 1) * BANK)
                 acc = psum.tile([P, BANK], F32, name="acc", tag="acc")
@@ -173,42 +209,50 @@ def tile_list_carer_rota_match_kernel(
                     nc.tensor.matmul_mx(
                         out=acc[:], lhsT=w2_w[:, a, 2 * P * i : 2 * P * (i + 1)].bitcast(FP4X4),
                         lhsT_scale=w2_s[:, a, P * i : P * (i + 1)],
-                        rhs=v_w[a][:, n].bitcast(FP8X4), rhs_scale=v_s[a][:, n],
+                        rhs=v_w[a][:, n].bitcast(FP8X4), rhs_scale=(v_s, v_s_low)[a][:, n],
                         start=(a == 0), stop=(a == PASSES - 1),
                     )
                 g_sums[i].append(acc)
             for half in range(S // BANK):
                 n = slice(half * BANK, (half + 1) * BANK)
                 nc.vector.tensor_tensor(h[i][:, n], h_sums[half][:], base_sb[i][:, n], ALU.add)
+            if i == 0:
+                take_look(i)
             tanh_h[i] = ring.tile([P, S], F32, name="tanh_h", tag="tanh_h", bufs=2)
             nc.scalar.activation(out=tanh_h[i][:], in_=h[i][:], func=ACT.Tanh)
-            look[i] = ring.tile([P, M], F32, name="look", tag="look", bufs=2)
-            nc.scalar.activation(
-                out=look[i][:], in_=h[i][:].indirect(pos1_sb[:]), func=ACT.Sigmoid,
-                bias=rowvec["thr"][:, i : i + 1], scale=rowvec["steep"][:, i : i + 1],
-            )
+            if i > 0:
+                take_look(i)
 
-        def pair_terms(i):
+        g_sb = {}
+        half_m = M // 2
+
+        def second_result(i):
             b, t = divmod(i, PACK)
-            g = ring.tile([P, S], F32, name="g", tag="g", bufs=2)
+            g_sb[i] = ring.tile([P, S], F32, name="g", tag="g", bufs=2)
             for half in range(S // BANK):
                 n = slice(half * BANK, (half + 1) * BANK)
                 nc.vector.scalar_tensor_tensor(
-                    g[:, n], tanh_h[i][:, n], rowvec["gain"][:, i : i + 1], g_sums[i][half][:], ALU.mult, ALU.add
+                    g_sb[i][:, n], tanh_h[i][:, n], rowvec["gain"][:, i : i + 1], g_sums[i][half][:],
+                    ALU.mult, ALU.add,
                 )
-            nc.vector.tensor_tensor(diff[b][:, t, :], look[i][:], diff[b][:, t, :], ALU.subtract)
-            nc.vector.tensor_copy(picked[b][:, t, :], g[:].indirect(pos2_sb[:]))
+            nc.vector.tensor_tensor(diff[i][:], look[i][:], diff[i][:], ALU.subtract)
+
+        def pick(i):
+            b, t = divmod(i, PACK)
+            if t == 0:
+                f_sb[b] = ring.tile([P, PACK, M], F32, name="f_sb", tag="group", bufs=3)
+            nc.vector.tensor_tensor(f_sb[b][:, t, :], g_sb[i][:].indirect(pos2_sb[:]), diff[i][:], ALU.mult)
 
         def by_lines(ap_t_m):
             return ap_t_m.rearrange("p t (c i) -> p c t i", i=PACK)
 
-        def woven(rounded):
-            return rounded[:].rearrange("p (c i t) -> p c t i", i=PACK, t=PACK)
+        def woven(rounded_ap):
+            return rounded_ap.rearrange("p (c i t) -> p c t i", i=PACK, t=PACK)
 
-        def quantize_f(b):
-            rounded = rounded_tile()
-            nc.vector.tensor_tensor(woven(rounded), by_lines(diff[b][:]), by_lines(picked[b][:]), ALU.mult)
-            f_q[b] = quantize("f_%d" % b, rounded)
+        f_q = {}
+
+        def round_f(copy, rounded, b, m0, m1):
+            copy(out=woven(rounded[:, PACK * m0 : PACK * m1]), in_=by_lines(f_sb[b][:, :, m0:m1]))
 
         tiles = H // P
         load_later(0)
@@ -216,56 +260,62 @@ def tile_list_carer_rota_match_kernel(
         for i in range(tiles):
             if i + 2 < tiles:
                 load_rows(i + 2)
+            if i == 0:
+                load_w2_words(1)
             if 1 <= i <= 4:
                 load_later(i + 1)
             first_products(i)
             if i >= 1:
-                pair_terms(i - 1)
-            if i == PACK:
-                quantize_f(0)
-            if i < 2:
-                prepare_later(i)
-            if 3 <= i < 7:
+                second_result(i - 1)
+                pick(i - 1)
+            if i in (1, 2):
                 prepare_later(i - 1)
+            if i in (4, 6):
+                prepare_later(i // 2)
+            if i == 5:
+                rounded = rounded_tile()
+                round_f(nc.scalar.copy, rounded, 0, 0, half_m)
+                round_f(nc.scalar.copy, rounded, 0, half_m, M)
+                f_q[0] = quantize("f_0", rounded)
+        second_result(tiles - 1)
+        pick(tiles - 1)
 
-        y_sums = {}
-
-        def last_pass(g, t, b):
-            cols = slice(t * P, (t + 1) * P)
-            if b == 0:
-                y_sums[g, t] = psum.tile([P, BANK], F32, name="acc", tag="acc")
-            codes, scales = w3_q[b, g]
-            nc.tensor.matmul_mx(
-                out=y_sums[g, t][:], lhsT=codes[:, cols].bitcast(FP8X4), lhsT_scale=scales[:, cols],
-                rhs=f_q[b][0][:].bitcast(FP8X4), rhs_scale=f_q[b][1][:],
-                start=(b == 0), stop=(b == PASSES - 1),
-            )
-
-        for t in range(PACK):
-            last_pass(0, t, 0)
-        pair_terms(tiles - 1)
-        for t in range(PACK):
-            last_pass(1, t, 0)
-        quantize_f(1)
         y_rows = out_0.rearrange("(g p t) m -> g p t m", p=P, t=PACK)
         y_scales = keep.tile([P, PASSES, M], U8, name="y_scales", align_bytes=64)
+        y_codes = keep.tile([P, PASSES, M], U32, name="y_codes", align_bytes=64)
+        rounded = rounded_tile()
+        round_f(nc.scalar.copy, rounded, 1, 0, SCALAR_SHARE)
+        round_f(nc.vector.tensor_copy, rounded, 1, SCALAR_SHARE, M)
+        f_q[1] = quantize("f_1", rounded)
+        prepare_later(4)
+        prepare_later(5)
         for g in range(PASSES):
-            y = ring.tile([P, PACK, M], F32, name="y", tag="group", bufs=4)
+            y = ring.tile([P, PACK, M], F32, name="y", tag="group", bufs=3)
             for t in range(PACK):
-                last_pass(g, t, 1)
+                cols = slice(t * P, (t + 1) * P)
+                acc = psum.tile([P, M], F32, name="acc", tag="acc")
+                for b in range(PASSES):
+                    codes, scales = w3_q[b, g]
+                    nc.tensor.matmul_mx(
+                        out=acc[:], lhsT=codes[:, cols].bitcast(FP8X4), lhsT_scale=scales[:, cols],
+                        rhs=f_q[b][0][:].bitcast(FP8X4), rhs_scale=f_q[b][1][:],
+                        start=(b == 0), stop=(b == PASSES - 1),
+                    )
                 col = rowvec["bias"][:, PACK * g + t : PACK * g + t + 1]
                 if g == 0 and t % 2 == 1:
-                    nc.vector.tensor_scalar_add(y[:, t, :], y_sums[g, t][:], col)
+                    nc.vector.tensor_scalar_add(y[:, t, :], acc[:], col)
                 else:
-                    nc.scalar.activation(out=y[:, t, :], in_=y_sums[g, t][:], func=ACT.Identity, bias=col)
+                    nc.scalar.activation(out=y[:, t, :], in_=acc[:], func=ACT.Identity, bias=col)
                 if t % 2 == 1:
                     nc.sync.dma_start(out=y_rows[g][:, t - 1 : t + 1, :], in_=y[:, t - 1 : t + 1, :])
             rounded = rounded_tile()
-            nc.vector.tensor_copy(out=woven(rounded), in_=by_lines(y[:]))
-            y_codes = keep.tile([P, M], U32, name="y_codes%d" % g, align_bytes=64)
-            nc.vector.quantize_mx(out=y_codes[:].bitcast(FP8X4), scales=y_scales[:, g, :], in_=rounded[:])
+            m0 = SCALAR_SHARE if g == PASSES - 1 else 0
+            if m0:
+                nc.scalar.copy(out=woven(rounded[:, : PACK * m0]), in_=by_lines(y[:, :, :m0]))
+            nc.vector.tensor_copy(out=woven(rounded[:, PACK * m0 :]), in_=by_lines(y[:, :, m0:]))
+            nc.vector.quantize_mx(out=y_codes[:, g, :].bitcast(FP8X4), scales=y_scales[:, g, :], in_=rounded[:])
             nc.sync.dma_start(
-                out=out_1[g].rearrange("p m t -> p (m t)").bitcast(I32), in_=y_codes[:].bitcast(I32)
+                out=out_1[g].rearrange("p m t -> p (m t)").bitcast(I32), in_=y_codes[:, g, :].bitcast(I32)
             )
         for q in range(QUADS):
             sb, dram = plane_rows(y_scales, out_2, q)

@@ -39,10 +39,9 @@ def tile_list_carer_rota_match_kernel(
         pos1_sb = keep.tile([P, M // 16], U16, name="pos1_sb")
         pos2_sb = keep.tile([P, M // 16], U16, name="pos2_sb")
         tab_w = [keep.tile([P, T], U32, name="tab_w%d" % a) for a in range(PASSES)]
-        tab_s = keep.tile([P, T], U8, name="tab_s")
+        tab_s = keep.tile([P, PASSES, T], U8, name="tab_s")
         v_w = [keep.tile([P, S], U32, name="v_w%d" % a, align_bytes=64) for a in range(PASSES)]
-        v_s = keep.tile([P, S], U8, name="v_s", align_bytes=64)
-        v_s_low = keep.tile([P, S], U8, name="v_s_low", align_bytes=64)
+        v_s = [keep.tile([P, S], U8, name="v_s%d" % a, align_bytes=64) for a in range(PASSES)]
         w2_w_raw = [keep.tile([P, PASSES, 2 * PASS], U8, name="w2_w_raw%d" % b) for b in range(PASSES)]
         w2_s_raw = keep.tile([P, PASSES, H], U8, name="w2_s_raw")
         w2_w = keep.tile([P, PASSES, 2 * H], U8, name="w2_w", align_bytes=64)
@@ -68,11 +67,13 @@ def tile_list_carer_rota_match_kernel(
             )
 
         def rounded_tile():
-            return ring.tile([P, PACK * PASS], BF16, name="rounded", tag="rounded", bufs=4, align_bytes=64)
+            return ring.tile([P, PACK * PASS], BF16, name="rounded", tag="rounded", bufs=3, align_bytes=64)
 
-        def quantize(name, rounded):
-            codes = keep.tile([P, PASS], U32, name=name + "_w", align_bytes=64)
-            scales = keep.tile([P, PASS], U8, name=name + "_s", align_bytes=64)
+        def quantize(name, rounded, codes=None, scales=None):
+            if codes is None:
+                codes = keep.tile([P, PASS], U32, name=name + "_w", align_bytes=64)
+            if scales is None:
+                scales = keep.tile([P, PASS], U8, name=name + "_s", align_bytes=64)
             nc.vector.quantize_mx(out=codes[:].bitcast(FP8X4), scales=scales[:], in_=rounded[:])
             return codes, scales
 
@@ -112,37 +113,34 @@ def tile_list_carer_rota_match_kernel(
             )
 
         nc.vector.memset(tab_s[:].bitcast(I32), 0)
-        nc.vector.memset(w2_s_raw[:].bitcast(I32), 0)
-        nc.vector.memset(v_s_low[:].bitcast(I32), 0)
-        for r in range(QUADS):
-            sb, dram = plane_rows(w2_s_raw, w2_scales, r)
-            nc.gpsimd.dma_start(out=sb, in_=dram)
+        nc.gpsimd.memset(w2_s_raw[:].bitcast(I32), 0)
         nc.sync.dma_start(offs_sb[:], offs)
         nc.sync.dma_start(pos1_sb[:], pos1)
         nc.sync.dma_start(pos2_sb[:], pos2)
         for name, vec in (("gain", gain), ("steep", steep), ("thr", thr), ("bias", bias)):
             load_vector(name, vec)
         load_table(0)
-        for q in range(QUADS):
-            nc.sync.dma_start(
-                out=tab_s[32 * q : 32 * q + 8, :].bitcast(I32), in_=tab_scales[:, 4 * q : 4 * q + 4, :].bitcast(I32)
-            )
+        for r in range(QUADS):
+            sb, dram = plane_rows(tab_s, tab_scales, r)
+            nc.sync.dma_start(out=sb, in_=dram)
         load_table(1)
         raw00 = load_weight(w1, 0, 0)
         raw10 = load_weight(w1, 1, 0)
         load_base(0)
         load_w2_words(0)
+        for r in range(QUADS):
+            sb, dram = plane_rows(w2_s_raw, w2_scales, r)
+            nc.sync.dma_start(out=sb, in_=dram)
         load_base(1)
         load_pref(0)
         load_pref(1)
 
         w1_q, w3_q = {}, {}
         nc.vector.tensor_copy(v_w[0][:], tab_w[0][:].indirect(offs_sb[:]))
-        nc.vector.tensor_copy(v_s[:], tab_s[:].indirect(offs_sb[:]))
-        for r in range(QUADS):
-            nc.gpsimd.dma_start(out=v_s_low[r:P:32, :].bitcast(I32), in_=v_s[4 + r : P : 32, :].bitcast(I32))
+        for a in range(PASSES):
+            nc.vector.tensor_copy(v_s[a][:], tab_s[:, a, :].indirect(offs_sb[:]))
         nc.vector.tensor_copy(v_w[1][:], tab_w[1][:].indirect(offs_sb[:]))
-        for a, raw, split in ((0, raw00, 64), (1, raw10, 44)):
+        for a, raw, split in ((0, raw00, 96), (1, raw10, 44)):
             rounded = rounded_tile()
             round_weight(nc.scalar.copy, rounded, raw, 0, split)
             round_weight(nc.vector.tensor_copy, rounded, raw, split, P)
@@ -167,12 +165,13 @@ def tile_list_carer_rota_match_kernel(
             store, name, w, k_group, col_group = later[n]
             later_raw[n] = load_weight(w, k_group, col_group)
 
-        def prepare_later(n):
+        def prepare_later(n, rounded=None, codes=None):
             store, name, w, k_group, col_group = later[n]
-            rounded = rounded_tile()
+            if rounded is None:
+                rounded = rounded_tile()
             round_weight(nc.scalar.copy, rounded, later_raw[n], 0, P // 2)
             round_weight(nc.scalar.copy, rounded, later_raw[n], P // 2, P)
-            store[k_group, col_group] = quantize("%s_%d%d" % (name, k_group, col_group), rounded)
+            store[k_group, col_group] = quantize("%s_%d%d" % (name, k_group, col_group), rounded, codes)
 
         h, tanh_h, look, g_sums = {}, {}, {}, {}
 
@@ -186,7 +185,10 @@ def tile_list_carer_rota_match_kernel(
         def first_products(i):
             b, t = divmod(i, PACK)
             cols = slice(t * P, (t + 1) * P)
-            h[i] = ring.tile([P, S], F32, name="h", tag="h", bufs=3)
+            if i < H // P - 1:
+                h[i] = ring.tile([P, S], F32, name="h", tag="h", bufs=3)
+            else:
+                h[i] = ring.tile([P, S], F32, name="h", tag="h_last", bufs=1, align_bytes=64)
             h_sums = []
             g_sums[i] = []
             for half in range(S // BANK):
@@ -196,7 +198,7 @@ def tile_list_carer_rota_match_kernel(
                     codes, scales = w1_q[a, b]
                     nc.tensor.matmul_mx(
                         out=acc[:], lhsT=codes[:, cols].bitcast(FP8X4), lhsT_scale=scales[:, cols],
-                        rhs=v_w[a][:, n].bitcast(FP8X4), rhs_scale=v_s[4 * a : P, n],
+                        rhs=v_w[a][:, n].bitcast(FP8X4), rhs_scale=v_s[a][:, n],
                         start=(a == 0), stop=(a == PASSES - 1),
                     )
                 h_sums.append(acc)
@@ -209,7 +211,7 @@ def tile_list_carer_rota_match_kernel(
                     nc.tensor.matmul_mx(
                         out=acc[:], lhsT=w2_w[:, a, 2 * P * i : 2 * P * (i + 1)].bitcast(FP4X4),
                         lhsT_scale=w2_s[:, a, P * i : P * (i + 1)],
-                        rhs=v_w[a][:, n].bitcast(FP8X4), rhs_scale=(v_s, v_s_low)[a][:, n],
+                        rhs=v_w[a][:, n].bitcast(FP8X4), rhs_scale=v_s[a][:, n],
                         start=(a == 0), stop=(a == PASSES - 1),
                     )
                 g_sums[i].append(acc)
@@ -218,7 +220,7 @@ def tile_list_carer_rota_match_kernel(
                 nc.vector.tensor_tensor(h[i][:, n], h_sums[half][:], base_sb[i][:, n], ALU.add)
             if i == 0:
                 take_look(i)
-            tanh_h[i] = ring.tile([P, S], F32, name="tanh_h", tag="tanh_h", bufs=2)
+            tanh_h[i] = ring.tile([P, S], F32, name="tanh_h", tag="tanh_h", bufs=2, align_bytes=64)
             nc.scalar.activation(out=tanh_h[i][:], in_=h[i][:], func=ACT.Tanh)
             if i > 0:
                 take_look(i)
@@ -273,34 +275,47 @@ def tile_list_carer_rota_match_kernel(
             if i in (4, 6):
                 prepare_later(i // 2)
             if i == 5:
-                rounded = rounded_tile()
-                round_f(nc.scalar.copy, rounded, 0, 0, half_m)
-                round_f(nc.scalar.copy, rounded, 0, half_m, M)
-                f_q[0] = quantize("f_0", rounded)
+                f0_rounded = keep.tile([P, PACK * M], BF16, name="f0_rounded", align_bytes=64)
+                round_f(nc.scalar.copy, f0_rounded, 0, 0, half_m)
+                round_f(nc.scalar.copy, f0_rounded, 0, half_m, M)
+        y_sums = {}
+
+        def last_pass(g, t, b):
+            cols = slice(t * P, (t + 1) * P)
+            if b == 0:
+                y_sums[g, t] = psum.tile([P, M], F32, name="acc", tag="acc")
+            codes, scales = w3_q[b, g]
+            nc.tensor.matmul_mx(
+                out=y_sums[g, t][:], lhsT=codes[:, cols].bitcast(FP8X4), lhsT_scale=scales[:, cols],
+                rhs=f_q[b][0][:].bitcast(FP8X4), rhs_scale=f_q[b][1][:],
+                start=(b == 0), stop=(b == PASSES - 1),
+            )
+
         second_result(tiles - 1)
+        f0_codes = ring.tile([P, M], U32, name="f0_codes", tag="tanh_h", bufs=2, align_bytes=64)
+        f0_scales = ring.tile([P, M], U8, name="f0_scales", tag="tanh_h", bufs=2, align_bytes=64)
+        f_q[0] = quantize("f_0", f0_rounded, f0_codes, f0_scales)
         pick(tiles - 1)
+        for t in range(PACK):
+            last_pass(0, t, 0)
+        late = ring.tile([P, PASSES, PACK * PASS], BF16, name="late", tag="h_last", bufs=1, align_bytes=64)
+        prepare_later(4, late[:, 0, :])
+        for t in range(PACK):
+            last_pass(1, t, 0)
 
         y_rows = out_0.rearrange("(g p t) m -> g p t m", p=P, t=PACK)
         y_scales = keep.tile([P, PASSES, M], U8, name="y_scales", align_bytes=64)
         y_codes = keep.tile([P, PASSES, M], U32, name="y_codes", align_bytes=64)
-        rounded = rounded_tile()
-        round_f(nc.scalar.copy, rounded, 1, 0, SCALAR_SHARE)
-        round_f(nc.vector.tensor_copy, rounded, 1, SCALAR_SHARE, M)
+        rounded = ring.tile([P, PACK * M], BF16, name="f1_rounded", tag="f1_rounded", bufs=1, align_bytes=64)
+        round_f(nc.vector.tensor_copy, rounded, 1, 0, M)
         f_q[1] = quantize("f_1", rounded)
-        prepare_later(4)
-        prepare_later(5)
+        last_codes = ring.tile([P, PASS], U32, name="last_codes", tag="f1_rounded", bufs=1, align_bytes=64)
+        prepare_later(5, late[:, 1, :], last_codes)
         for g in range(PASSES):
             y = ring.tile([P, PACK, M], F32, name="y", tag="group", bufs=3)
             for t in range(PACK):
-                cols = slice(t * P, (t + 1) * P)
-                acc = psum.tile([P, M], F32, name="acc", tag="acc")
-                for b in range(PASSES):
-                    codes, scales = w3_q[b, g]
-                    nc.tensor.matmul_mx(
-                        out=acc[:], lhsT=codes[:, cols].bitcast(FP8X4), lhsT_scale=scales[:, cols],
-                        rhs=f_q[b][0][:].bitcast(FP8X4), rhs_scale=f_q[b][1][:],
-                        start=(b == 0), stop=(b == PASSES - 1),
-                    )
+                last_pass(g, t, 1)
+                acc = y_sums[g, t]
                 col = rowvec["bias"][:, PACK * g + t : PACK * g + t + 1]
                 if g == 0 and t % 2 == 1:
                     nc.vector.tensor_scalar_add(y[:, t, :], acc[:], col)

@@ -48,7 +48,11 @@ def tile_list_carer_rota_match_kernel(
         w2_s = keep.tile([P, PASSES, H], U8, name="w2_s", align_bytes=64)
         rowvec = {}
         for name in ("gain", "steep", "thr", "bias"):
-            rowvec[name] = keep.tile([P, PASSES * PACK], F32, name=name + "_sb")
+            rowvec[name] = keep.tile([P, PASSES, 2 * PACK], F32, name=name + "_sb")
+
+        def row_value(name, i):
+            b, t = divmod(i, PACK)
+            return rowvec[name][:, b, t : t + 1]
 
         def plane_rows(tile, dram, r):
             sb = tile[r:P:32, :, :].bitcast(I32)
@@ -60,10 +64,10 @@ def tile_list_carer_rota_match_kernel(
             nc.sync.dma_start(out=raw[:], in_=rows.rearrange("(p j) c -> p j c", j=PACK))
             return raw
 
-        def round_weight(copy, rounded, raw, m0, m1):
+        def round_weight(copy, rounded, raw, m0, m1, t0=0, t1=PACK):
             copy(
-                out=rounded[:].rearrange("p (t m j) -> p m j t", t=PACK, j=PACK)[:, m0:m1],
-                in_=raw[:].rearrange("p j (m t) -> p m j t", t=PACK)[:, m0:m1],
+                out=rounded[:].rearrange("p (t m j) -> p m j t", t=PACK, j=PACK)[:, m0:m1, :, t0:t1],
+                in_=raw[:].rearrange("p j (m t) -> p m j t", t=PACK)[:, m0:m1, :, t0:t1],
             )
 
         def rounded_tile():
@@ -96,15 +100,16 @@ def tile_list_carer_rota_match_kernel(
             load_pref(i)
 
         def load_vector(name, vec):
-            nc.sync.dma_start(
-                out=rowvec[name][:].rearrange("p (b t) -> p b t", t=PACK),
+            nc.scalar.dma_start(
+                out=rowvec[name][:, :, :PACK],
                 in_=vec.rearrange("(b p t) -> p b t", p=P, t=PACK),
             )
 
-        def load_table(a):
-            nc.sync.dma_start(
-                out=tab_w[a][:].bitcast(I32), in_=tab_words[a].rearrange("p t i -> p (t i)").bitcast(I32)
-            )
+        def load_table(a, pieces):
+            words = tab_words[a].rearrange("p t i -> p (t i)").bitcast(I32)
+            for c0 in range(0, T, T // pieces):
+                cols = slice(c0, c0 + T // pieces)
+                nc.sync.dma_start(out=tab_w[a][:, cols].bitcast(I32), in_=words[:, cols])
 
         def load_w2_words(b):
             cols = slice(b * PASS // 2, (b + 1) * PASS // 2)
@@ -115,23 +120,23 @@ def tile_list_carer_rota_match_kernel(
         nc.vector.memset(tab_s[:].bitcast(I32), 0)
         nc.gpsimd.memset(w2_s_raw[:].bitcast(I32), 0)
         nc.sync.dma_start(offs_sb[:], offs)
-        nc.sync.dma_start(pos1_sb[:], pos1)
-        nc.sync.dma_start(pos2_sb[:], pos2)
-        for name, vec in (("gain", gain), ("steep", steep), ("thr", thr), ("bias", bias)):
+        load_table(0, 4)
+        for name, vec in (("steep", steep), ("thr", thr), ("gain", gain), ("bias", bias)):
             load_vector(name, vec)
-        load_table(0)
         for r in range(QUADS):
             sb, dram = plane_rows(tab_s, tab_scales, r)
             nc.sync.dma_start(out=sb, in_=dram)
-        load_table(1)
+        load_table(1, 1)
         raw00 = load_weight(w1, 0, 0)
         raw10 = load_weight(w1, 1, 0)
         load_base(0)
+        nc.sync.dma_start(pos1_sb[:], pos1)
         load_w2_words(0)
         for r in range(QUADS):
             sb, dram = plane_rows(w2_s_raw, w2_scales, r)
             nc.sync.dma_start(out=sb, in_=dram)
         load_base(1)
+        nc.sync.dma_start(pos2_sb[:], pos2)
         load_pref(0)
         load_pref(1)
 
@@ -169,8 +174,8 @@ def tile_list_carer_rota_match_kernel(
             store, name, w, k_group, col_group = later[n]
             if rounded is None:
                 rounded = rounded_tile()
-            round_weight(nc.scalar.copy, rounded, later_raw[n], 0, P // 2)
-            round_weight(nc.scalar.copy, rounded, later_raw[n], P // 2, P)
+            round_weight(nc.scalar.copy, rounded, later_raw[n], 0, P, 0, 2)
+            round_weight(nc.scalar.copy, rounded, later_raw[n], 0, P, 2, PACK)
             store[k_group, col_group] = quantize("%s_%d%d" % (name, k_group, col_group), rounded, codes)
 
         h, tanh_h, look, g_sums = {}, {}, {}, {}
@@ -179,7 +184,7 @@ def tile_list_carer_rota_match_kernel(
             look[i] = ring.tile([P, M], F32, name="look", tag="look", bufs=3)
             nc.scalar.activation(
                 out=look[i][:], in_=h[i][:].indirect(pos1_sb[:]), func=ACT.Sigmoid,
-                bias=rowvec["thr"][:, i : i + 1], scale=rowvec["steep"][:, i : i + 1],
+                bias=row_value("thr", i), scale=row_value("steep", i),
             )
 
         def first_products(i):
@@ -234,7 +239,7 @@ def tile_list_carer_rota_match_kernel(
             for half in range(S // BANK):
                 n = slice(half * BANK, (half + 1) * BANK)
                 nc.vector.scalar_tensor_tensor(
-                    g_sb[i][:, n], tanh_h[i][:, n], rowvec["gain"][:, i : i + 1], g_sums[i][half][:],
+                    g_sb[i][:, n], tanh_h[i][:, n], row_value("gain", i), g_sums[i][half][:],
                     ALU.mult, ALU.add,
                 )
             nc.vector.tensor_tensor(diff[i][:], look[i][:], diff[i][:], ALU.subtract)
@@ -316,7 +321,7 @@ def tile_list_carer_rota_match_kernel(
             for t in range(PACK):
                 last_pass(g, t, 1)
                 acc = y_sums[g, t]
-                col = rowvec["bias"][:, PACK * g + t : PACK * g + t + 1]
+                col = row_value("bias", PACK * g + t)
                 if g == 0 and t % 2 == 1:
                     nc.vector.tensor_scalar_add(y[:, t, :], acc[:], col)
                 else:

from contextlib import ExitStack

import concourse.mybir as mybir

K, H, N, T, S, M = 1024, 1024, 1024, 4096, 1024, 512
FLOPS = 2 * (2 * K * H * S + H * N * M)

F32 = mybir.dt.float32
BF16 = mybir.dt.bfloat16
I32 = mybir.dt.int32
U32 = mybir.dt.uint32
U16 = mybir.dt.uint16
U8 = mybir.dt.uint8
FP8X4 = mybir.dt.float8_e4m3fn_x4
FP4X4 = mybir.dt.float4_e2m1fn_x4
ACT = mybir.ActivationFunctionType
ALU = mybir.AluOpType

P = 128
PACK = 4
PASS = P * PACK
PASSES = 2
BANK = 512
QUADS = 4
SCALAR_SHARE = 176


def tile_list_carer_rota_match_kernel(
    tc, tab_words, tab_scales, offs, pos1, pos2, w1, base, w2_words, w2_scales,
    gain, steep, thr, pref, w3, bias, out_0, out_1, out_2,
):
    nc = tc.nc
    with ExitStack() as ctx:
        keep = ctx.enter_context(tc.tile_pool(name="keep", bufs=1))
        ring = ctx.enter_context(tc.tile_pool(name="ring", bufs=2))
        psum = ctx.enter_context(tc.psum_pool(name="psum", bufs=8))

        offs_sb = keep.tile([P, S // 16], U16, name="offs_sb")
        pos1_sb = keep.tile([P, M // 16], U16, name="pos1_sb")
        pos2_sb = keep.tile([P, M // 16], U16, name="pos2_sb")
        tab_w = [keep.tile([P, T], U32, name="tab_w%d" % a) for a in range(PASSES)]
        tab_s = keep.tile([P, PASSES, T], U8, name="tab_s")
        v_w = [keep.tile([P, S], U32, name="v_w%d" % a, align_bytes=64) for a in range(PASSES)]
        v_s = [keep.tile([P, S], U8, name="v_s%d" % a, align_bytes=64) for a in range(PASSES)]
        w2_w_raw = [keep.tile([P, PASSES, 2 * PASS], U8, name="w2_w_raw%d" % b) for b in range(PASSES)]
        w2_s_raw = keep.tile([P, PASSES, H], U8, name="w2_s_raw")
        w2_w = keep.tile([P, PASSES, 2 * H], U8, name="w2_w", align_bytes=64)
        w2_s = keep.tile([P, PASSES, H], U8, name="w2_s", align_bytes=64)
        rowvec = {}
        for name in ("gain", "steep", "thr", "bias"):
            rowvec[name] = keep.tile([P, PASSES, 2 * PACK], F32, name=name + "_sb")

        def row_value(name, i):
            b, t = divmod(i, PACK)
            return rowvec[name][:, b, t : t + 1]

        def plane_rows(tile, dram, r):
            sb = tile[r:P:32, :, :].bitcast(I32)
            return sb, dram[:, r : 16 : 4, :].bitcast(I32).rearrange("a q n -> q a n")

        def load_weight(w, k_group, col_group):
            raw = ring.tile([P, PACK, PASS], F32, name="raw", tag="raw", bufs=4)
            rows = w[k_group * PASS : (k_group + 1) * PASS, col_group * PASS : (col_group + 1) * PASS]
            nc.sync.dma_start(out=raw[:], in_=rows.rearrange("(p j) c -> p j c", j=PACK))
            return raw

        def round_weight(copy, rounded, raw, m0, m1, t0=0, t1=PACK):
            copy(
                out=rounded[:].rearrange("p (t m j) -> p m j t", t=PACK, j=PACK)[:, m0:m1, :, t0:t1],
                in_=raw[:].rearrange("p j (m t) -> p m j t", t=PACK)[:, m0:m1, :, t0:t1],
            )

        def rounded_tile():
            return ring.tile([P, PACK * PASS], BF16, name="rounded", tag="rounded", bufs=3, align_bytes=64)

        def quantize(name, rounded, codes=None, scales=None):
            if codes is None:
                codes = keep.tile([P, PASS], U32, name=name + "_w", align_bytes=64)
            if scales is None:
                scales = keep.tile([P, PASS], U8, name=name + "_s", align_bytes=64)
            nc.vector.quantize_mx(out=codes[:].bitcast(FP8X4), scales=scales[:], in_=rounded[:])
            return codes, scales

        base_rows = base.rearrange("(b p t) n -> b t p n", p=P, t=PACK)
        pref_rows = pref.rearrange("(b p t) n -> b t p n", p=P, t=PACK)
        base_sb, diff, f_sb = {}, {}, {}

        def load_base(i):
            b, t = divmod(i, PACK)
            base_sb[i] = ring.tile([P, S], F32, name="base_sb", tag="base_sb", bufs=4)
            nc.sync.dma_start(out=base_sb[i][:], in_=base_rows[b, t])

        def load_pref(i):
            b, t = divmod(i, PACK)
            diff[i] = ring.tile([P, M], F32, name="diff", tag="diff", bufs=4)
            nc.sync.dma_start(out=diff[i][:], in_=pref_rows[b, t])

        def load_rows(i):
            load_base(i)
            load_pref(i)

        def load_vector(name, vec):
            nc.scalar.dma_start(
                out=rowvec[name][:, :, :PACK],
                in_=vec.rearrange("(b p t) -> p b t", p=P, t=PACK),
            )

        def load_table(a, pieces):
            words = tab_words[a].rearrange("p t i -> p (t i)").bitcast(I32)
            for c0 in range(0, T, T // pieces):
                cols = slice(c0, c0 + T // pieces)
                nc.sync.dma_start(out=tab_w[a][:, cols].bitcast(I32), in_=words[:, cols])

        def load_w2_words(b):
            cols = slice(b * PASS // 2, (b + 1) * PASS // 2)
            nc.sync.dma_start(
                out=w2_w_raw[b][:].bitcast(I32), in_=w2_words.bitcast(I32).rearrange("a p n -> p a n")[:, :, cols]
            )

        nc.vector.memset(tab_s[:].bitcast(I32), 0)
        nc.gpsimd.memset(w2_s_raw[:].bitcast(I32), 0)
        nc.sync.dma_start(offs_sb[:], offs)
        load_table(0, 4)
        for name, vec in (("steep", steep), ("thr", thr), ("gain", gain), ("bias", bias)):
            load_vector(name, vec)
        for r in range(QUADS):
            sb, dram = plane_rows(tab_s, tab_scales, r)
            nc.sync.dma_start(out=sb, in_=dram)
        load_table(1, 1)
        raw00 = load_weight(w1, 0, 0)
        raw10 = load_weight(w1, 1, 0)
        load_base(0)
        nc.sync.dma_start(pos1_sb[:], pos1)
        load_w2_words(0)
        for r in range(QUADS):
            sb, dram = plane_rows(w2_s_raw, w2_scales, r)
            nc.sync.dma_start(out=sb, in_=dram)
        load_base(1)
        nc.sync.dma_start(pos2_sb[:], pos2)
        load_pref(0)
        load_pref(1)

        w1_q, w3_q = {}, {}
        nc.vector.tensor_copy(v_w[0][:], tab_w[0][:].indirect(offs_sb[:]))
        for a in range(PASSES):
            nc.vector.tensor_copy(v_s[a][:], tab_s[:, a, :].indirect(offs_sb[:]))
        nc.vector.tensor_copy(v_w[1][:], tab_w[1][:].indirect(offs_sb[:]))
        for a, raw, split in ((0, raw00, 96), (1, raw10, 44)):
            rounded = rounded_tile()
            round_weight(nc.scalar.copy, rounded, raw, 0, split)
            round_weight(nc.vector.tensor_copy, rounded, raw, split, P)
            w1_q[a, 0] = quantize("w1_%d0" % a, rounded)

        def deal_w2(b):
            cols = slice(b * PASS, (b + 1) * PASS)
            nc.scalar.copy(
                out=w2_w[:].bitcast(U16)[:, :, cols].rearrange("p a (t m) -> p a t m", t=PACK),
                in_=w2_w_raw[b][:].bitcast(U16).rearrange("p a (m t) -> p a t m", t=PACK),
            )
            nc.vector.tensor_copy(
                out=w2_s[:, :, cols].rearrange("p a (t m) -> p a t m", t=PACK),
                in_=w2_s_raw[:, :, cols].rearrange("p a (m t) -> p a t m", t=PACK),
            )

        later = [(w1_q, "w1", w1, a, 1) for a in range(PASSES)]
        later = later + [(w3_q, "w3", w3, b, g) for g in range(PASSES) for b in range(PASSES)]
        later_raw = {}

        def load_later(n):
            store, name, w, k_group, col_group = later[n]
            later_raw[n] = load_weight(w, k_group, col_group)

        def prepare_later(n, rounded=None, codes=None):
            store, name, w, k_group, col_group = later[n]
            if rounded is None:
                rounded = rounded_tile()
            round_weight(nc.scalar.copy, rounded, later_raw[n], 0, P, 0, 2)
            round_weight(nc.scalar.copy, rounded, later_raw[n], 0, P, 2, PACK)
            store[k_group, col_group] = quantize("%s_%d%d" % (name, k_group, col_group), rounded, codes)

        h, tanh_h, look, g_sums = {}, {}, {}, {}

        def take_look(i):
            look[i] = ring.tile([P, M], F32, name="look", tag="look", bufs=3)
            nc.scalar.activation(
                out=look[i][:], in_=h[i][:].indirect(pos1_sb[:]), func=ACT.Sigmoid,
                bias=row_value("thr", i), scale=row_value("steep", i),
            )

        def first_products(i):
            b, t = divmod(i, PACK)
            cols = slice(t * P, (t + 1) * P)
            if i < H // P - 1:
                h[i] = ring.tile([P, S], F32, name="h", tag="h", bufs=3)
            else:
                h[i] = ring.tile([P, S], F32, name="h", tag="h_last", bufs=1, align_bytes=64)
            h_sums = []
            g_sums[i] = []
            for half in range(S // BANK):
                n = slice(half * BANK, (half + 1) * BANK)
                acc = psum.tile([P, BANK], F32, name="acc", tag="acc")
                for a in range(PASSES):
                    codes, scales = w1_q[a, b]
                    nc.tensor.matmul_mx(
                        out=acc[:], lhsT=codes[:, cols].bitcast(FP8X4), lhsT_scale=scales[:, cols],
                        rhs=v_w[a][:, n].bitcast(FP8X4), rhs_scale=v_s[a][:, n],
                        start=(a == 0), stop=(a == PASSES - 1),
                    )
                h_sums.append(acc)
            if t == 0:
                deal_w2(b)
            for half in range(S // BANK):
                n = slice(half * BANK, (half + 1) * BANK)
                acc = psum.tile([P, BANK], F32, name="acc", tag="acc")
                for a in range(PASSES):
                    nc.tensor.matmul_mx(
                        out=acc[:], lhsT=w2_w[:, a, 2 * P * i : 2 * P * (i + 1)].bitcast(FP4X4),
                        lhsT_scale=w2_s[:, a, P * i : P * (i + 1)],
                        rhs=v_w[a][:, n].bitcast(FP8X4), rhs_scale=v_s[a][:, n],
                        start=(a == 0), stop=(a == PASSES - 1),
                    )
                g_sums[i].append(acc)
            for half in range(S // BANK):
                n = slice(half * BANK, (half + 1) * BANK)
                nc.vector.tensor_tensor(h[i][:, n], h_sums[half][:], base_sb[i][:, n], ALU.add)
            if i == 0:
                take_look(i)
            tanh_h[i] = ring.tile([P, S], F32, name="tanh_h", tag="tanh_h", bufs=2, align_bytes=64)
            nc.scalar.activation(out=tanh_h[i][:], in_=h[i][:], func=ACT.Tanh)
            if i > 0:
                take_look(i)

        g_sb = {}
        half_m = M // 2

        def second_result(i):
            b, t = divmod(i, PACK)
            g_sb[i] = ring.tile([P, S], F32, name="g", tag="g", bufs=2)
            for half in range(S // BANK):
                n = slice(half * BANK, (half + 1) * BANK)
                nc.vector.scalar_tensor_tensor(
                    g_sb[i][:, n], tanh_h[i][:, n], row_value("gain", i), g_sums[i][half][:],
                    ALU.mult, ALU.add,
                )
            nc.vector.tensor_tensor(diff[i][:], look[i][:], diff[i][:], ALU.subtract)

        def pick(i):
            b, t = divmod(i, PACK)
            if t == 0:
                f_sb[b] = ring.tile([P, PACK, M], F32, name="f_sb", tag="group", bufs=3)
            nc.vector.tensor_tensor(f_sb[b][:, t, :], g_sb[i][:].indirect(pos2_sb[:]), diff[i][:], ALU.mult)

        def by_lines(ap_t_m):
            return ap_t_m.rearrange("p t (c i) -> p c t i", i=PACK)

        def woven(rounded_ap):
            return rounded_ap.rearrange("p (c i t) -> p c t i", i=PACK, t=PACK)

        f_q = {}

        def round_f(copy, rounded, b, m0, m1):
            copy(out=woven(rounded[:, PACK * m0 : PACK * m1]), in_=by_lines(f_sb[b][:, :, m0:m1]))

        tiles = H // P
        load_later(0)
        load_later(1)
        for i in range(tiles):
            if i + 2 < tiles:
                load_rows(i + 2)
            if i == 0:
                load_w2_words(1)
            if 1 <= i <= 4:
                load_later(i + 1)
            first_products(i)
            if i >= 1:
                second_result(i - 1)
                pick(i - 1)
            if i in (1, 2):
                prepare_later(i - 1)
            if i in (4, 6):
                prepare_later(i // 2)
            if i == 5:
                f0_rounded = keep.tile([P, PACK * M], BF16, name="f0_rounded", align_bytes=64)
                round_f(nc.scalar.copy, f0_rounded, 0, 0, half_m)
                round_f(nc.scalar.copy, f0_rounded, 0, half_m, M)
        y_sums = {}

        def last_pass(g, t, b):
            cols = slice(t * P, (t + 1) * P)
            if b == 0:
                y_sums[g, t] = psum.tile([P, M], F32, name="acc", tag="acc")
            codes, scales = w3_q[b, g]
            nc.tensor.matmul_mx(
                out=y_sums[g, t][:], lhsT=codes[:, cols].bitcast(FP8X4), lhsT_scale=scales[:, cols],
                rhs=f_q[b][0][:].bitcast(FP8X4), rhs_scale=f_q[b][1][:],
                start=(b == 0), stop=(b == PASSES - 1),
            )

        second_result(tiles - 1)
        f0_codes = ring.tile([P, M], U32, name="f0_codes", tag="tanh_h", bufs=2, align_bytes=64)
        f0_scales = ring.tile([P, M], U8, name="f0_scales", tag="tanh_h", bufs=2, align_bytes=64)
        f_q[0] = quantize("f_0", f0_rounded, f0_codes, f0_scales)
        pick(tiles - 1)
        for t in range(PACK):
            last_pass(0, t, 0)
        late = ring.tile([P, PASSES, PACK * PASS], BF16, name="late", tag="h_last", bufs=1, align_bytes=64)
        prepare_later(4, late[:, 0, :])
        for t in range(PACK):
            last_pass(1, t, 0)

        y_rows = out_0.rearrange("(g p t) m -> g p t m", p=P, t=PACK)
        y_scales = keep.tile([P, PASSES, M], U8, name="y_scales", align_bytes=64)
        y_codes = keep.tile([P, PASSES, M], U32, name="y_codes", align_bytes=64)
        rounded = ring.tile([P, PACK * M], BF16, name="f1_rounded", tag="f1_rounded", bufs=1, align_bytes=64)
        round_f(nc.vector.tensor_copy, rounded, 1, 0, M)
        f_q[1] = quantize("f_1", rounded)
        last_codes = ring.tile([P, PASS], U32, name="last_codes", tag="f1_rounded", bufs=1, align_bytes=64)
        prepare_later(5, late[:, 1, :], last_codes)
        for g in range(PASSES):
            y = ring.tile([P, PACK, M], F32, name="y", tag="group", bufs=3)
            for t in range(PACK):
                last_pass(g, t, 1)
                acc = y_sums[g, t]
                col = row_value("bias", PACK * g + t)
                if g == 0 and t % 2 == 1:
                    nc.vector.tensor_scalar_add(y[:, t, :], acc[:], col)
                else:
                    nc.scalar.activation(out=y[:, t, :], in_=acc[:], func=ACT.Identity, bias=col)
                if t % 2 == 1:
                    nc.sync.dma_start(out=y_rows[g][:, t - 1 : t + 1, :], in_=y[:, t - 1 : t + 1, :])
            rounded = rounded_tile()
            m0 = SCALAR_SHARE if g == PASSES - 1 else 0
            if m0:
                nc.scalar.copy(out=woven(rounded[:, : PACK * m0]), in_=by_lines(y[:, :, :m0]))
            nc.vector.tensor_copy(out=woven(rounded[:, PACK * m0 :]), in_=by_lines(y[:, :, m0:]))
            nc.vector.quantize_mx(out=y_codes[:, g, :].bitcast(FP8X4), scales=y_scales[:, g, :], in_=rounded[:])
            nc.sync.dma_start(
                out=out_1[g].rearrange("p m t -> p (m t)").bitcast(I32), in_=y_codes[:, g, :].bitcast(I32)
            )
        for q in range(QUADS):
            sb, dram = plane_rows(y_scales, out_2, q)
            engine = nc.scalar if q % 2 == 0 else nc.sync
            engine.dma_start(out=dram, in_=sb)
